import numpy as np
import ml_dtypes


def mxq(x, axis, fmt="e4m3"):
    dtype, down = {"e4m3": (ml_dtypes.float8_e4m3fn, 7), "e5m2": (ml_dtypes.float8_e5m2, 14)}[fmt]
    v = np.moveaxis(np.asarray(x, np.float32).astype(ml_dtypes.bfloat16).astype(np.float64), axis, -1)
    blocks = v.reshape(v.shape[:-1] + (-1, 32))
    amax = np.abs(blocks).max(-1, keepdims=True)
    byte = np.maximum(np.where(amax > 0, np.frexp(amax)[1] - 1 + 127, 0) - down, 1)
    scale = np.exp2(byte - 127.0)
    codes = (blocks / scale).astype(np.float32).astype(dtype).astype(np.float64)
    return np.moveaxis((codes * scale).reshape(v.shape), -1, axis)


WIDE = False


def mx_kscale(k):
    if not WIDE:
        return np.ones(k)
    levels = np.array([10, -10, 5, -5, 0])
    if k % 512:
        return np.exp2(np.random.permutation(np.resize(levels, k // 32))).repeat(32)
    a = np.empty((k // 512, 16))
    for p in range(k // 512):
        a[p, :8] = np.random.permutation(np.resize(levels, 8))
        for g in range(8):
            far = levels[np.abs(levels - a[p, g]) >= 10]
            a[p, g + 8] = far[np.random.randint(len(far))]
    return np.exp2(a.ravel()).repeat(32)


def f64(x):
    return np.asarray(x).astype(np.float64)


def striped(idx):
    return np.tile(idx.reshape(-1, 16).T, (8, 1)).astype(np.uint16)


def unstriped(offs):
    return offs[:16].T.reshape(-1).astype(np.int64)


E2M1 = np.array([0.0, 0.5, 1.0, 1.5, 2.0, 3.0, 4.0, 6.0, -0.0, -0.5, -1.0, -1.5, -2.0, -3.0, -4.0, -6.0])


def pack_weight(w, fmt):
    k, n = w.shape
    w = f64(np.asarray(w, np.float32).astype(ml_dtypes.bfloat16)).reshape(k // 32, 32, n)
    amax = np.abs(w).max(1)
    if fmt == "e4m3":
        byte = np.frexp(amax)[1] - 1 + 127 - 7
    else:
        mant, ex = np.frexp(amax / 6.0)
        byte = np.where(mant > 0.5, ex, ex - 1) + 127
    byte = np.clip(np.where(amax > 0, byte, 1), 1, 254)
    scaled = (w * np.exp2(127.0 - byte)[:, None, :]).reshape(k, n).astype(np.float32)
    by_word = np.ascontiguousarray(scaled.reshape(k // 512, 128, 4, n).transpose(0, 1, 3, 2))
    if fmt == "e4m3":
        words = by_word.astype(ml_dtypes.float8_e4m3fn).view(np.uint8)
    else:
        c = by_word.astype(ml_dtypes.float4_e2m1fn).view(np.uint8) & 0xF
        words = (c[..., 0::2] | (c[..., 1::2] << 4)).reshape(k // 512, 128, 2 * n)
    return np.ascontiguousarray(words), np.ascontiguousarray(byte.astype(np.uint8).reshape(k // 512, 16, n))


def unpack_weight(words, scales, fmt):
    g, _, n = scales.shape
    words = np.ascontiguousarray(words).reshape(g, 128, n, -1)
    if fmt == "e4m3":
        vals = words.view(ml_dtypes.float8_e4m3fn).astype(np.float64)
    else:
        nib = np.empty((g, 128, n, 4), np.uint8)
        nib[..., 0::2] = words & 0xF
        nib[..., 1::2] = words >> 4
        vals = E2M1[nib]
    vals = vals * np.repeat(np.exp2(scales.astype(np.float64) - 127.0), 8, axis=1)[..., None]
    return vals.transpose(0, 1, 3, 2).reshape(g * 512, n)


def gelu(v):
    return 0.5 * v * (1.0 + np.tanh(np.sqrt(2.0 / np.pi) * (v + 0.044715 * v**3)))


def striped8(idx):
    return np.concatenate([v.reshape(-1, 16).T for v in idx]).astype(np.uint16)


def unstriped8(offs):
    return np.stack([offs[16 * g:16 * g + 16].T.reshape(-1) for g in range(8)]).astype(np.int64)


def heads(h, wgt, idx8):
    r = np.arange(h.shape[0])
    return wgt[r // 4 % 128] * h[r[:, None], idx8[r % 512 // 64]]


def put_heads(h, wgs, idx8, t2):
    r = np.arange(h.shape[0])
    page = np.zeros((h.shape[0], t2))
    page[r[:, None], idx8[r % 512 // 64]] = wgs[r // 4 % 128] * h
    return page


K, H, N, T, S, P, T2 = 1024, 1024, 512, 4096, 1024, 1024, 2048

def setup_inputs():
    n = np.random.standard_normal
    s, u = mx_kscale(K)[:, None], mx_kscale(H)[:, None]
    d = {}
    d["tab_words"], d["tab_scales"] = pack_weight(n((K, T)) * s, "e4m3")
    d["offs"] = striped(np.random.permutation(T)[:S])
    d["offs2"] = striped8(np.stack([np.random.permutation(T2)[:S] for _ in range(8)]))
    d["offs3"] = striped8(np.stack([np.random.permutation(T2)[:P] for _ in range(8)]))
    d["w1"] = (n((K, H)) / s / K ** 0.5).astype(np.float32)
    d["effort"] = np.exp(0.3 * n(H)).astype(np.float32)
    d["wgs"] = np.repeat(np.random.uniform(0.5, 2.0, (8, S)), 16, axis=0).astype(np.float32)
    d["wgt"] = np.repeat(np.random.uniform(0.5, 2.0, (8, P)), 16, axis=0).astype(np.float32)
    d["relief"] = (np.exp(0.3 * n(H)) * u[:, 0]).astype(np.float32)
    d["pain"] = (0.7 * n((H, P)) * u).astype(np.float32)
    d["wa_words"], d["wa_scales"] = pack_weight(n((H, N)) / u / H ** 0.5, "e2m1")
    d["wb"] = (n((H, N)) / u / H ** 0.5).astype(np.float32)
    d["ba"] = (0.7 * n(N)).astype(np.float32)
    return d

def reference(tab_words, tab_scales, offs, offs2, offs3, w1, effort, wgs, wgt, relief, pain, wa_words, wa_scales, wb, ba):
    v = unpack_weight(tab_words, tab_scales, "e4m3")[:, unstriped(offs)]
    h = (mxq(f64(w1), 0, "e4m3").T @ v) * f64(effort)[:, None]
    page = put_heads(h, f64(wgs), unstriped8(offs2), T2)
    x = heads(page, f64(wgt), unstriped8(offs3))
    act = x / (1.0 + np.exp(-x))
    z = act * f64(relief)[:, None] + f64(pain)
    zq = mxq(z, 0, "e4m3")
    ya = unpack_weight(wa_words, wa_scales, "e2m1").T @ zq
    yb = mxq(f64(wb), 0, "e4m3").T @ zq
    return np.minimum(ya + f64(ba)[:, None], yb)

@@ -1,0 +1,289 @@
+from contextlib import ExitStack
+
+import concourse.mybir as mybir
+
+K, H, N, T, S, M, T2 = 1024, 1024, 512, 4096, 1024, 1024, 2048
+FLOPS = 2 * K * H * S + 2 * 2 * H * N * M
+
+F32 = mybir.dt.float32
+BF16 = mybir.dt.bfloat16
+I32 = mybir.dt.int32
+U32 = mybir.dt.uint32
+U16 = mybir.dt.uint16
+U8 = mybir.dt.uint8
+FP8X4 = mybir.dt.float8_e4m3fn_x4
+FP4X4 = mybir.dt.float4_e2m1fn_x4
+ALU = mybir.AluOpType
+ACT = mybir.ActivationFunctionType
+
+P = 128
+PACK = 4
+KP = P * PACK
+PASSES = 2
+SLICES = PASSES * PACK
+BANK = 512
+PAGES = 3
+CHUNK = (1024, 256)
+YW = 256
+
+
+def tile_list_shoulder_recovery_scores_kernel(
+    tc, tab_words, tab_scales, offs, offs2, offs3, w1, effort, wgs, wgt, relief, pain, wa_words, wa_scales, wb, ba, out
+):
+    nc = tc.nc
+    with ExitStack() as ctx:
+        lists = ctx.enter_context(tc.tile_pool(name="lists", bufs=1))
+        keep = ctx.enter_context(tc.tile_pool(name="keep", bufs=1))
+        ring = ctx.enter_context(tc.tile_pool(name="ring", bufs=2))
+        psum = ctx.enter_context(tc.psum_pool(name="psum", bufs=8))
+
+        idx = lists.tile([P, S // 16], U16, name="idx")
+        idx2 = lists.tile([P, S // 16], U16, name="idx2")
+        idx3 = lists.tile([P, M // 16], U16, name="idx3")
+
+        tab_s = keep.tile([P, T], U8, name="tab_s", align_bytes=64)
+        wa_s = keep.tile([P, PASSES, N], U8, name="wa_s", align_bytes=64)
+        pages = [keep.tile([P, T2], F32, name=f"page{j}") for j in range(PAGES)]
+        nc.vector.memset(tab_s[:].bitcast(I32), 0)
+        nc.vector.memset(wa_s[:].rearrange("p a n -> p (a n)").bitcast(I32), 0)
+        for page in pages:
+            nc.vector.memset(page[:], 0.0)
+
+        def load_table_words(a):
+            words = ring.tile([P, T], U32, name=f"tab_w{a}", tag="big")
+            nc.sync.dma_start(words[:].bitcast(I32), tab_words[a].rearrange("p t i -> p (t i)").bitcast(I32))
+            return words
+
+        def load_rows(src, a, c0):
+            raw = ring.tile([P, PACK, KP], F32, name="raw", tag="raw", bufs=3)
+            nc.sync.dma_start(raw[:], src[KP * a : KP * (a + 1), c0 : c0 + KP].rearrange("(p j) c -> p j c", j=PACK))
+            return raw
+
+        nc.sync.dma_start(idx[:], offs)
+        tab_w = [load_table_words(0)]
+        for q in range(4):
+            nc.sync.dma_start(
+                tab_s[32 * q : 32 * q + 4 * PASSES, :].bitcast(I32), tab_scales[:, 4 * q : 4 * q + 4, :].bitcast(I32)
+            )
+        tab_w.append(load_table_words(1))
+        w1_raw = {}
+        for a in range(PASSES):
+            w1_raw[a, 0] = load_rows(w1, a, 0)
+        effort_t = keep.tile([P, PASSES, PACK], F32, name="effort_t")
+        nc.sync.dma_start(effort_t[:], effort.rearrange("(b p i) -> p b i", b=PASSES, i=PACK))
+        nc.sync.dma_start(idx2[:], offs2)
+        wgs_t = keep.tile([P, S], F32, name="wgs_t")
+        nc.sync.dma_start(wgs_t[:], wgs)
+        nc.sync.dma_start(idx3[:], offs3)
+        wgt_t = keep.tile([P, M], F32, name="wgt_t")
+        nc.sync.dma_start(wgt_t[:], wgt)
+        relief_t = keep.tile([P, PASSES, PACK], F32, name="relief_t")
+        nc.sync.dma_start(relief_t[:], relief.rearrange("(b p i) -> p b i", b=PASSES, i=PACK))
+
+        v_w = [keep.tile([P, S], U32, name=f"v_w{a}", align_bytes=64) for a in range(PASSES)]
+        v_s = keep.tile([P, S], U8, name="v_s", align_bytes=64)
+        nc.vector.tensor_copy(v_w[0][:], tab_w[0][:].indirect(idx[:]))
+        nc.vector.tensor_copy(v_s[:], tab_s[:].indirect(idx[:]))
+        nc.vector.tensor_copy(v_w[1][:], tab_w[1][:].indirect(idx[:]))
+
+        def quantize(grouped, width, name):
+            codes = keep.tile([P, width], U32, name=name + "_w", align_bytes=64)
+            scales = keep.tile([P, width], U8, name=name + "_s", align_bytes=64)
+            nc.vector.quantize_mx(out=codes[:].bitcast(FP8X4), scales=scales[:], in_=grouped)
+            return codes, scales
+
+        def round_w1(a, b, u):
+            grouped = ring.tile([P, PACK * KP], BF16, name="grouped", tag="grouped", bufs=3, align_bytes=64)
+            dst = grouped[:, : 2 * KP].rearrange("p (e m j) -> p m j e", e=2, j=PACK)
+            src = w1_raw[a, b][:].rearrange("p j (m i) -> p m j i", i=PACK)[:, :, :, 2 * u : 2 * u + 2]
+            if (b, u) == (0, 0):
+                nc.vector.tensor_copy(dst, src)
+            else:
+                nc.scalar.copy(dst, src)
+            return grouped
+
+        w1_q = {}
+
+        def prepare_w1(b, u):
+            for a in range(PASSES):
+                grouped = round_w1(a, b, u)
+                w1_q[a, b, u] = quantize(grouped[:, : 2 * KP], 2 * P, f"w1q{a}{b}{u}")
+
+        def features(s):
+            b, i = divmod(s, PACK)
+            h = ring.tile([P, S], F32, name="h", tag="h", bufs=3)
+            for c0 in range(0, S, BANK):
+                cols = slice(c0, c0 + BANK)
+                acc = psum.tile([P, BANK], F32, name="acc", tag="bank")
+                for a in range(PASSES):
+                    codes, scales = w1_q[a, b, i // 2]
+                    rows = slice(P * (i % 2), P * (i % 2 + 1))
+                    nc.tensor.matmul_mx(
+                        out=acc[:],
+                        lhsT=codes[:, rows].bitcast(FP8X4),
+                        lhsT_scale=scales[:, rows],
+                        rhs=v_w[a][:, cols].bitcast(FP8X4),
+                        rhs_scale=v_s[4 * a :, cols],
+                        start=(a == 0),
+                        stop=(a == PASSES - 1),
+                    )
+                nc.scalar.activation(h[:, cols], acc[:], ACT.Copy, scale=effort_t[:, b, i : i + 1])
+            return h
+
+        def put(s, h):
+            nc.vector.tensor_tensor(pages[s % PAGES][:].indirect(idx2[:]), h[:], wgs_t[:], ALU.mult)
+
+        act = [
+            [keep.tile([P, PACK, CHUNK[b]], F32, name=f"act{b}_{c0}") for c0 in range(0, M, CHUNK[b])] for b in range(PASSES)
+        ]
+
+        def read(s, c0, width):
+            b, i = divmod(s, PACK)
+            x = ring.tile([P, width], F32, name="x", tag="x")
+            offsets = idx3[:, c0 // 16 : (c0 + width) // 16]
+            nc.vector.tensor_tensor(x[:], pages[s % PAGES][:].indirect(offsets), wgt_t[:, c0 : c0 + width], ALU.mult)
+            sil = ring.tile([P, width], F32, name="sil", tag="sil")
+            nc.scalar.activation(sil[:], x[:], ACT.Silu)
+            for d0 in range(0, width, CHUNK[b]):
+                nc.scalar.activation(
+                    act[b][(c0 + d0) // CHUNK[b]][:, i, :], sil[:, d0 : d0 + CHUNK[b]], ACT.Copy, scale=relief_t[:, b, i : i + 1]
+                )
+
+        pain_t = []
+        z_q = {}
+
+        def make_z(b, c):
+            width = CHUNK[b]
+            zb = keep.tile([P, width * PACK], BF16, name=f"zb{b}_{c}", align_bytes=64)
+            nc.vector.tensor_tensor(
+                zb[:].rearrange("p (m e i) -> p m i e", e=2, i=PACK),
+                act[b][c][:].rearrange("p i (m e) -> p m i e", e=2),
+                pain_t[b][:, :, c * width : (c + 1) * width].rearrange("p i (m e) -> p m i e", e=2),
+                ALU.add,
+            )
+            return zb
+
+        def quantize_z(b, c, zb):
+            z_q[b, c] = quantize(zb[:], CHUNK[b], f"zq{b}_{c}")
+
+        prepare_w1(0, 0)
+        h = {0: features(0)}
+        h[1] = features(1)
+        prepare_w1(0, 1)
+
+        for a in range(PASSES):
+            w1_raw[a, 1] = load_rows(w1, a, KP)
+        for b in range(PASSES):
+            rows = ring.tile([P, PACK, M], F32, name=f"pain{b}", tag="big")
+            nc.sync.dma_start(rows[:], pain[KP * b : KP * (b + 1), :].rearrange("(p i) m -> p i m", i=PACK))
+            pain_t.append(rows)
+        wb_raw = [load_rows(wb, b, 0) for b in range(PASSES)]
+        wa_w = keep.tile([P, PASSES, 2 * N], U8, name="wa_w", align_bytes=64)
+        nc.sync.dma_start(wa_w[:].bitcast(I32), wa_words.rearrange("a p c -> p a c").bitcast(I32))
+        for q in range(4):
+            nc.sync.dma_start(
+                wa_s[32 * q : 32 * q + 4, :, :].bitcast(I32),
+                wa_scales[:, 4 * q : 4 * q + 4, :].rearrange("a r c -> r a c").bitcast(I32),
+            )
+        ba_t = keep.tile([P, N // P], F32, name="ba_t")
+        with nc.allow_non_contiguous_dma(reason="one bias value a partition"):
+            nc.sync.dma_start(ba_t[:], ba.rearrange("(t p) -> p t", p=P))
+
+        wb_q = []
+
+        def prepare_wb(b):
+            grouped = ring.tile([P, PACK * KP], BF16, name="grouped", tag="grouped", bufs=3, align_bytes=64)
+            nc.scalar.copy(
+                grouped[:].rearrange("p (n e j) -> p n j e", e=2, j=PACK),
+                wb_raw[b][:].rearrange("p j (n e) -> p n j e", e=2),
+            )
+            wb_q.append(quantize(grouped[:], N, f"wbq{b}"))
+
+        put(0, h[0])
+        for s in range(1, SLICES):
+            if s + 1 < SLICES:
+                h[s + 1] = features(s + 1)
+            put(s, h[s])
+            read(s - 1, 0, M)
+            if s == 1:
+                prepare_w1(1, 0)
+            if s == 2:
+                prepare_w1(1, 1)
+            if s == 3:
+                prepare_wb(0)
+            if s == 4:
+                prepare_wb(1)
+            if s == 5:
+                zb0 = make_z(0, 0)
+            if s == 6:
+                quantize_z(0, 0, zb0)
+
+        chunks = M // YW
+        banks = {}
+
+        def z_operand(b, c, lo, width):
+            per = CHUNK[b] // YW
+            codes, scales = z_q[b, c // per]
+            cols = slice((c % per) * YW + lo, (c % per) * YW + lo + width)
+            return codes[:, cols].bitcast(FP8X4), scales[:, cols]
+
+        def products(b, c):
+            for pair in range(2):
+                if b == 0:
+                    banks[c, pair] = [psum.tile([P, 2, YW], F32, name=name, tag="bank") for name in ("ya", "yb")]
+                ya, yb = banks[c, pair]
+                for j in range(2):
+                    n0 = P * (2 * pair + j)
+                    for lo in range(0, YW, P):
+                        rhs, rhs_scale = z_operand(b, c, lo, P)
+                        nc.tensor.matmul_mx(
+                            out=ya[:, j, lo : lo + P],
+                            lhsT=wa_w[:, b, 2 * n0 : 2 * (n0 + P)].bitcast(FP4X4),
+                            lhsT_scale=wa_s[:, b, n0 : n0 + P],
+                            rhs=rhs,
+                            rhs_scale=rhs_scale,
+                            start=(b == 0 and j == 0 and lo == 0),
+                            stop=(b == PASSES - 1 and j == 1 and lo == YW - P),
+                        )
+                for j in range(2):
+                    n0 = P * (2 * pair + j)
+                    rhs, rhs_scale = z_operand(b, c, 0, YW)
+                    nc.tensor.matmul_mx(
+                        out=yb[:, j, :],
+                        lhsT=wb_q[b][0][:, n0 : n0 + P].bitcast(FP8X4),
+                        lhsT_scale=wb_q[b][1][:, n0 : n0 + P],
+                        rhs=rhs,
+                        rhs_scale=rhs_scale,
+                        start=(b == 0 and j == 0),
+                        stop=(b == PASSES - 1 and j == 1),
+                    )
+
+        def finish(c):
+            for pair in range(2):
+                ya, yb = banks[c, pair]
+                biased = ring.tile([P, 2, YW], F32, name="biased", tag="biased")
+                for j in range(2):
+                    t = 2 * pair + j
+                    nc.scalar.activation(biased[:, j, :], ya[:, j, :], ACT.Identity, bias=ba_t[:, t : t + 1])
+                result = ring.tile([P, 2, YW], F32, name="result", tag="result", bufs=3)
+                nc.vector.tensor_tensor(result[:], yb[:], biased[:], ALU.min)
+                nc.sync.dma_start(
+                    out[2 * P * pair : 2 * P * (pair + 1), c * YW : (c + 1) * YW].rearrange("(j p) m -> p j m", p=P), result[:]
+                )
+
+        products(0, 0)
+        products(0, 1)
+        last = SLICES - 1
+        zb = {}
+        for step in range(chunks + 3):
+            if step < chunks:
+                read(last, step * YW, YW)
+            if 0 <= step - 2 < chunks:
+                quantize_z(1, step - 2, zb[step - 2])
+                if step - 2 >= 2:
+                    products(0, step - 2)
+                products(1, step - 2)
+            if 0 <= step - 1 < chunks:
+                zb[step - 1] = make_z(1, step - 1)
+            if 0 <= step - 3 < chunks:
+                finish(step - 3)

@@ -1,6 +1,7 @@
 from contextlib import ExitStack
 
 import concourse.mybir as mybir
+from concourse.masks import make_identity
 
 K, H, N, T, S, M, T2 = 1024, 1024, 512, 4096, 1024, 1024, 2048
 FLOPS = 2 * K * H * S + 2 * 2 * H * N * M
@@ -44,10 +45,14 @@ def tile_list_shoulder_recovery_scores_kernel(
         tab_s = keep.tile([P, T], U8, name="tab_s", align_bytes=64)
         wa_s = keep.tile([P, PASSES, N], U8, name="wa_s", align_bytes=64)
         pages = [keep.tile([P, T2], F32, name=f"page{j}") for j in range(PAGES)]
-        nc.vector.memset(tab_s[:].bitcast(I32), 0)
+        v_s = keep.tile([P, PASSES, S], U8, name="v_s", align_bytes=64)
+        nc.vector.memset(tab_s[32:64, :].bitcast(I32), 0)
+        nc.vector.memset(tab_s[64:, :].bitcast(I32), 0)
+        nc.vector.memset(v_s[:].rearrange("p a n -> p (a n)").bitcast(I32), 0)
         nc.vector.memset(wa_s[:].rearrange("p a n -> p (a n)").bitcast(I32), 0)
-        for page in pages:
-            nc.vector.memset(page[:], 0.0)
+        nc.vector.memset(pages[0][:], 0.0)
+        for page in pages[1:]:
+            nc.gpsimd.memset(page[:], 0.0)
 
         def load_table_words(a):
             words = ring.tile([P, T], U32, name=f"tab_w{a}", tag="big")
@@ -60,12 +65,8 @@ def tile_list_shoulder_recovery_scores_kernel(
             return raw
 
         nc.sync.dma_start(idx[:], offs)
-        tab_w = [load_table_words(0)]
-        for q in range(4):
-            nc.sync.dma_start(
-                tab_s[32 * q : 32 * q + 4 * PASSES, :].bitcast(I32), tab_scales[:, 4 * q : 4 * q + 4, :].bitcast(I32)
-            )
-        tab_w.append(load_table_words(1))
+        nc.sync.dma_start(tab_s[:32, :].bitcast(I32), tab_scales.rearrange("a q t -> q a t").bitcast(I32))
+        tab_w = [load_table_words(a) for a in range(PASSES)]
         w1_raw = {}
         for a in range(PASSES):
             w1_raw[a, 0] = load_rows(w1, a, 0)
@@ -81,10 +82,14 @@ def tile_list_shoulder_recovery_scores_kernel(
         nc.sync.dma_start(relief_t[:], relief.rearrange("(b p i) -> p b i", b=PASSES, i=PACK))
 
         v_w = [keep.tile([P, S], U32, name=f"v_w{a}", align_bytes=64) for a in range(PASSES)]
-        v_s = keep.tile([P, S], U8, name="v_s", align_bytes=64)
-        nc.vector.tensor_copy(v_w[0][:], tab_w[0][:].indirect(idx[:]))
-        nc.vector.tensor_copy(v_s[:], tab_s[:].indirect(idx[:]))
-        nc.vector.tensor_copy(v_w[1][:], tab_w[1][:].indirect(idx[:]))
+        picked_s = keep.tile([P, S], U8, name="picked_s", align_bytes=64)
+        nc.vector.tensor_copy(picked_s[:], tab_s[:].indirect(idx[:]))
+        for q in range(4):
+            nc.scalar.dma_start(
+                v_s[32 * q : 32 * q + 4, :, :].bitcast(I32), picked_s[8 * q : 8 * q + 8, :].bitcast(I32)
+            )
+        for a in range(PASSES):
+            nc.vector.tensor_copy(v_w[a][:], tab_w[a][:].indirect(idx[:]))
 
         def quantize(grouped, width, name):
             codes = keep.tile([P, width], U32, name=name + "_w", align_bytes=64)
@@ -92,38 +97,44 @@ def tile_list_shoulder_recovery_scores_kernel(
             nc.vector.quantize_mx(out=codes[:].bitcast(FP8X4), scales=scales[:], in_=grouped)
             return codes, scales
 
-        def round_w1(a, b, u):
-            grouped = ring.tile([P, PACK * KP], BF16, name="grouped", tag="grouped", bufs=3, align_bytes=64)
-            dst = grouped[:, : 2 * KP].rearrange("p (e m j) -> p m j e", e=2, j=PACK)
-            src = w1_raw[a, b][:].rearrange("p j (m i) -> p m j i", i=PACK)[:, :, :, 2 * u : 2 * u + 2]
-            if (b, u) == (0, 0):
-                nc.vector.tensor_copy(dst, src)
-            else:
-                nc.scalar.copy(dst, src)
-            return grouped
-
         w1_q = {}
 
         def prepare_w1(b, u):
+            head = (b, u) == (0, 0)
+            grouped = ring.tile([P, PASSES, 2 * KP], BF16, name="grouped", tag="grouped", align_bytes=64)
+            codes = keep.tile([P, PASSES, 2 * P], U32, name=f"w1q{b}{u}_w", align_bytes=64)
+            scales = keep.tile([P, PASSES, 2 * P], U8, name=f"w1q{b}{u}_s", align_bytes=64)
             for a in range(PASSES):
-                grouped = round_w1(a, b, u)
-                w1_q[a, b, u] = quantize(grouped[:, : 2 * KP], 2 * P, f"w1q{a}{b}{u}")
+                dst = grouped[:, a, :].rearrange("p (e m j) -> p m j e", e=2, j=PACK)
+                src = w1_raw[a, b][:].rearrange("p j (m i) -> p m j i", i=PACK)[:, :, :, 2 * u : 2 * u + 2]
+                if head:
+                    nc.vector.tensor_copy(dst, src)
+                    nc.vector.quantize_mx(out=codes[:, a, :].bitcast(FP8X4), scales=scales[:, a, :], in_=grouped[:, a, :])
+                else:
+                    nc.scalar.copy(dst, src)
+            if not head:
+                nc.vector.quantize_mx(
+                    out=codes[:].rearrange("p a c -> p (a c)").bitcast(FP8X4),
+                    scales=scales[:].rearrange("p a c -> p (a c)"),
+                    in_=grouped[:].rearrange("p a c -> p (a c)"),
+                )
+            w1_q[b, u] = codes, scales
 
         def features(s):
             b, i = divmod(s, PACK)
-            h = ring.tile([P, S], F32, name="h", tag="h", bufs=3)
+            h = ring.tile([P, S], F32, name="h", tag="h")
             for c0 in range(0, S, BANK):
                 cols = slice(c0, c0 + BANK)
                 acc = psum.tile([P, BANK], F32, name="acc", tag="bank")
                 for a in range(PASSES):
-                    codes, scales = w1_q[a, b, i // 2]
+                    codes, scales = w1_q[b, i // 2]
                     rows = slice(P * (i % 2), P * (i % 2 + 1))
                     nc.tensor.matmul_mx(
                         out=acc[:],
-                        lhsT=codes[:, rows].bitcast(FP8X4),
-                        lhsT_scale=scales[:, rows],
+                        lhsT=codes[:, a, rows].bitcast(FP8X4),
+                        lhsT_scale=scales[:, a, rows],
                         rhs=v_w[a][:, cols].bitcast(FP8X4),
-                        rhs_scale=v_s[4 * a :, cols],
+                        rhs_scale=v_s[:, a, cols],
                         start=(a == 0),
                         stop=(a == PASSES - 1),
                     )
@@ -131,34 +142,75 @@ def tile_list_shoulder_recovery_scores_kernel(
             return h
 
         def put(s, h):
-            nc.vector.tensor_tensor(pages[s % PAGES][:].indirect(idx2[:]), h[:], wgs_t[:], ALU.mult)
+            width = BANK if s == 0 else S
+            for c0 in range(0, S, width):
+                cols = slice(c0, c0 + width)
+                window = pages[s % PAGES][:].indirect(idx2[:, c0 // 16 : (c0 + width) // 16])
+                nc.vector.tensor_tensor(window, h[:, cols], wgs_t[:, cols], ALU.mult)
 
-        act = [
-            [keep.tile([P, PACK, CHUNK[b]], F32, name=f"act{b}_{c0}") for c0 in range(0, M, CHUNK[b])] for b in range(PASSES)
-        ]
-
-        def read(s, c0, width):
-            b, i = divmod(s, PACK)
-            x = ring.tile([P, width], F32, name="x", tag="x")
-            offsets = idx3[:, c0 // 16 : (c0 + width) // 16]
-            nc.vector.tensor_tensor(x[:], pages[s % PAGES][:].indirect(offsets), wgt_t[:, c0 : c0 + width], ALU.mult)
-            sil = ring.tile([P, width], F32, name="sil", tag="sil")
-            nc.scalar.activation(sil[:], x[:], ACT.Silu)
-            for d0 in range(0, width, CHUNK[b]):
-                nc.scalar.activation(
-                    act[b][(c0 + d0) // CHUNK[b]][:, i, :], sil[:, d0 : d0 + CHUNK[b]], ACT.Copy, scale=relief_t[:, b, i : i + 1]
-                )
-
+        act = [keep.tile([P, PACK, YW], F32, name=f"act{c0}") for c0 in range(0, M, YW)]
+        act0 = keep.tile([P, PACK, M], F32, name="act_first", tag="act_first")
+        ident = keep.tile([P, P], F32, name="ident")
+        make_identity(nc, ident[:])
+        turned = [keep.tile([P, M], F32, name=f"turned{u}", tag=f"turned{u}", align_bytes=64) for u in range(2)]
+        x_last = []
         pain_t = []
         z_q = {}
 
+        def read(s, c0, width):
+            b, i = divmod(s, PACK)
+            if s == SLICES - 1:
+                x = sil = x_last[0][:, c0 : c0 + width]
+            else:
+                x = keep.tile([P, M], F32, name=f"x{s}", tag="x_spare" if s == SLICES - 2 else "x")
+                if s > PACK:
+                    sil = keep.tile([P, M], F32, name=f"sil{s}", tag=f"turned{SLICES - 2 - s}", align_bytes=64)
+                else:
+                    sil = ring.tile([P, M], F32, name="sil", tag="sil")
+            window = pages[s % PAGES][:].indirect(idx3[:, c0 // 16 : (c0 + width) // 16])
+            nc.vector.tensor_tensor(x[:], window, wgt_t[:, c0 : c0 + width], ALU.mult)
+            nc.scalar.activation(sil[:], x[:], ACT.Silu)
+            gain = relief_t[:, b, i : i + 1]
+            if b == 0:
+                nc.scalar.activation(act0[:, i, :], sil[:], ACT.Copy, scale=gain)
+            else:
+                for d0 in range(0, width, YW):
+                    nc.scalar.activation(act[(c0 + d0) // YW][:, i, :], sil[:, d0 : d0 + YW], ACT.Copy, scale=gain)
+
+        def turn_pair(u):
+            for t0 in range(0, M, 2 * P):
+                sums = psum.tile([P, 2, 2, P], F32, name="sums", tag="bank")
+                for t in range(2):
+                    cols = slice(t0 + P * t, t0 + P * (t + 1))
+                    for e in range(2):
+                        for first, src in ((True, pain_t[0]), (False, act0)):
+                            nc.tensor.matmul(
+                                sums[:, t, e, :], src[:, 2 * u + e, cols], ident[:], start=first, stop=not first, is_transpose=True
+                            )
+                nc.scalar.copy(
+                    turned[u][:, t0 : t0 + 2 * P].bitcast(BF16).rearrange("m (t p e) -> m t p e", t=2, e=2),
+                    sums[:].rearrange("m t e p -> m t p e"),
+                )
+
+        def weave_z0():
+            zb = ring.tile([P, M * PACK], BF16, name="zb0", tag="grouped", align_bytes=64)
+            for t0 in range(0, M, 2 * P):
+                back = psum.tile([P, 2, 2, P], F32, name="back", tag="bank")
+                for t in range(2):
+                    for u in range(2):
+                        nc.tensor.transpose(back[:, t, u, :], turned[u][:, t0 + P * t : t0 + P * (t + 1)], ident[:])
+                nc.scalar.copy(
+                    zb[:, PACK * t0 : PACK * (t0 + 2 * P)].bitcast(F32).rearrange("p (t m u) -> p t m u", t=2, u=2),
+                    back[:].rearrange("p t u m -> p t m u"),
+                )
+            return zb
+
         def make_z(b, c):
-            width = CHUNK[b]
-            zb = keep.tile([P, width * PACK], BF16, name=f"zb{b}_{c}", align_bytes=64)
+            zb = keep.tile([P, YW * PACK], BF16, name=f"zb{b}_{c}", align_bytes=64)
             nc.vector.tensor_tensor(
                 zb[:].rearrange("p (m e i) -> p m i e", e=2, i=PACK),
-                act[b][c][:].rearrange("p i (m e) -> p m i e", e=2),
-                pain_t[b][:, :, c * width : (c + 1) * width].rearrange("p i (m e) -> p m i e", e=2),
+                act[c][:].rearrange("p i (m e) -> p m i e", e=2),
+                pain_t[b][:, :, c * YW : (c + 1) * YW].rearrange("p i (m e) -> p m i e", e=2),
                 ALU.add,
             )
             return zb
@@ -173,11 +225,13 @@ def tile_list_shoulder_recovery_scores_kernel(
 
         for a in range(PASSES):
             w1_raw[a, 1] = load_rows(w1, a, KP)
+        wb_raw = []
         for b in range(PASSES):
             rows = ring.tile([P, PACK, M], F32, name=f"pain{b}", tag="big")
             nc.sync.dma_start(rows[:], pain[KP * b : KP * (b + 1), :].rearrange("(p i) m -> p i m", i=PACK))
             pain_t.append(rows)
-        wb_raw = [load_rows(wb, b, 0) for b in range(PASSES)]
+            if b == 0:
+                wb_raw.extend(load_rows(wb, a, 0) for a in range(PASSES))
         wa_w = keep.tile([P, PASSES, 2 * N], U8, name="wa_w", align_bytes=64)
         nc.sync.dma_start(wa_w[:].bitcast(I32), wa_words.rearrange("a p c -> p a c").bitcast(I32))
         for q in range(4):
@@ -189,37 +243,37 @@ def tile_list_shoulder_recovery_scores_kernel(
         with nc.allow_non_contiguous_dma(reason="one bias value a partition"):
             nc.sync.dma_start(ba_t[:], ba.rearrange("(t p) -> p t", p=P))
 
-        wb_q = []
-
-        def prepare_wb(b):
-            grouped = ring.tile([P, PACK * KP], BF16, name="grouped", tag="grouped", bufs=3, align_bytes=64)
-            nc.scalar.copy(
-                grouped[:].rearrange("p (n e j) -> p n j e", e=2, j=PACK),
-                wb_raw[b][:].rearrange("p j (n e) -> p n j e", e=2),
-            )
-            wb_q.append(quantize(grouped[:], N, f"wbq{b}"))
+        def prepare_wb():
+            grouped = ring.tile([P, PASSES, PACK * N], BF16, name="wb_grouped", tag="grouped", align_bytes=64)
+            for b in range(PASSES):
+                nc.scalar.copy(
+                    grouped[:, b, :].rearrange("p (n e j) -> p n j e", e=2, j=PACK),
+                    wb_raw[b][:].rearrange("p j (n e) -> p n j e", e=2),
+                )
+            return quantize(grouped[:].rearrange("p b c -> p (b c)"), PASSES * N, "wbq")
 
         put(0, h[0])
         for s in range(1, SLICES):
             if s + 1 < SLICES:
                 h[s + 1] = features(s + 1)
+            if s == SLICES - 2:
+                turn_pair(1)
+                zb0 = weave_z0()
             put(s, h[s])
             read(s - 1, 0, M)
             if s == 1:
                 prepare_w1(1, 0)
-            if s == 2:
                 prepare_w1(1, 1)
+            if s == 2:
+                wb_w, wb_s = prepare_wb()
             if s == 3:
-                prepare_wb(0)
-            if s == 4:
-                prepare_wb(1)
-            if s == 5:
-                zb0 = make_z(0, 0)
-            if s == 6:
-                quantize_z(0, 0, zb0)
+                turn_pair(0)
+        quantize_z(0, 0, zb0)
+        x_last.append(keep.tile([P, M], F32, name="x_last", tag="turned1", align_bytes=64))
 
         chunks = M // YW
         banks = {}
+        scores = keep.tile([P, 2 * chunks, 2 * YW], F32, name="scores", tag="act_first")
 
         def z_operand(b, c, lo, width):
             per = CHUNK[b] // YW
@@ -250,8 +304,8 @@ def tile_list_shoulder_recovery_scores_kernel(
                     rhs, rhs_scale = z_operand(b, c, 0, YW)
                     nc.tensor.matmul_mx(
                         out=yb[:, j, :],
-                        lhsT=wb_q[b][0][:, n0 : n0 + P].bitcast(FP8X4),
-                        lhsT_scale=wb_q[b][1][:, n0 : n0 + P],
+                        lhsT=wb_w[:, N * b + n0 : N * b + n0 + P].bitcast(FP8X4),
+                        lhsT_scale=wb_s[:, N * b + n0 : N * b + n0 + P],
                         rhs=rhs,
                         rhs_scale=rhs_scale,
                         start=(b == 0 and j == 0),
@@ -261,29 +315,38 @@ def tile_list_shoulder_recovery_scores_kernel(
         def finish(c):
             for pair in range(2):
                 ya, yb = banks[c, pair]
-                biased = ring.tile([P, 2, YW], F32, name="biased", tag="biased")
+                biased = scores[:, 2 * c + pair, :].rearrange("p (j m) -> p j m", j=2)
                 for j in range(2):
                     t = 2 * pair + j
                     nc.scalar.activation(biased[:, j, :], ya[:, j, :], ACT.Identity, bias=ba_t[:, t : t + 1])
-                result = ring.tile([P, 2, YW], F32, name="result", tag="result", bufs=3)
-                nc.vector.tensor_tensor(result[:], yb[:], biased[:], ALU.min)
+                nc.vector.tensor_tensor(biased, yb[:], biased, ALU.min)
                 nc.sync.dma_start(
-                    out[2 * P * pair : 2 * P * (pair + 1), c * YW : (c + 1) * YW].rearrange("(j p) m -> p j m", p=P), result[:]
+                    out[2 * P * pair : 2 * P * (pair + 1), c * YW : (c + 1) * YW].rearrange("(j p) m -> p j m", p=P), biased
                 )
 
         products(0, 0)
         products(0, 1)
         last = SLICES - 1
         zb = {}
-        for step in range(chunks + 3):
-            if step < chunks:
-                read(last, step * YW, YW)
-            if 0 <= step - 2 < chunks:
-                quantize_z(1, step - 2, zb[step - 2])
-                if step - 2 >= 2:
-                    products(0, step - 2)
-                products(1, step - 2)
-            if 0 <= step - 1 < chunks:
-                zb[step - 1] = make_z(1, step - 1)
-            if 0 <= step - 3 < chunks:
-                finish(step - 3)
+
+        def close(c):
+            quantize_z(1, c, zb[c])
+            if c >= 2:
+                products(0, c)
+            products(1, c)
+
+        for c in range(3):
+            read(last, c * YW, YW)
+        zb[0] = make_z(1, 0)
+        read(last, 3 * YW, YW)
+        close(0)
+        zb[1] = make_z(1, 1)
+        close(1)
+        zb[2] = make_z(1, 2)
+        finish(0)
+        close(2)
+        finish(1)
+        zb[3] = make_z(1, 3)
+        close(3)
+        finish(2)
+        finish(3)

from contextlib import ExitStack

import concourse.mybir as mybir
from concourse.masks import make_identity

K, H, N, T, S, M, T2 = 1024, 1024, 512, 4096, 1024, 1024, 2048
FLOPS = 2 * K * H * S + 2 * 2 * H * N * M

F32 = mybir.dt.float32
BF16 = mybir.dt.bfloat16
I32 = mybir.dt.int32
U32 = mybir.dt.uint32
U16 = mybir.dt.uint16
U8 = mybir.dt.uint8
FP8X4 = mybir.dt.float8_e4m3fn_x4
FP4X4 = mybir.dt.float4_e2m1fn_x4
ALU = mybir.AluOpType
ACT = mybir.ActivationFunctionType

P = 128
PACK = 4
KP = P * PACK
PASSES = 2
SLICES = PASSES * PACK
BANK = 512
PAGES = 3
CHUNK = (1024, 256)
YW = 256


def tile_list_shoulder_recovery_scores_kernel(
    tc, tab_words, tab_scales, offs, offs2, offs3, w1, effort, wgs, wgt, relief, pain, wa_words, wa_scales, wb, ba, out
):
    nc = tc.nc
    with ExitStack() as ctx:
        lists = ctx.enter_context(tc.tile_pool(name="lists", bufs=1))
        keep = ctx.enter_context(tc.tile_pool(name="keep", bufs=1))
        ring = ctx.enter_context(tc.tile_pool(name="ring", bufs=2))
        psum = ctx.enter_context(tc.psum_pool(name="psum", bufs=8))

        idx = lists.tile([P, S // 16], U16, name="idx")
        idx2 = lists.tile([P, S // 16], U16, name="idx2")
        idx3 = lists.tile([P, M // 16], U16, name="idx3")

        tab_s = keep.tile([P, T], U8, name="tab_s", align_bytes=64)
        wa_s = keep.tile([P, PASSES, N], U8, name="wa_s", align_bytes=64)
        pages = [keep.tile([P, T2], F32, name=f"page{j}") for j in range(PAGES)]
        v_s = keep.tile([P, PASSES, S], U8, name="v_s", align_bytes=64)
        nc.vector.memset(tab_s[32:64, :].bitcast(I32), 0)
        nc.vector.memset(tab_s[64:, :].bitcast(I32), 0)
        nc.vector.memset(v_s[:].rearrange("p a n -> p (a n)").bitcast(I32), 0)
        nc.vector.memset(wa_s[:].rearrange("p a n -> p (a n)").bitcast(I32), 0)
        nc.vector.memset(pages[0][:], 0.0)
        for page in pages[1:]:
            nc.gpsimd.memset(page[:], 0.0)

        def load_table_words(a):
            words = ring.tile([P, T], U32, name=f"tab_w{a}", tag="big")
            nc.sync.dma_start(words[:].bitcast(I32), tab_words[a].rearrange("p t i -> p (t i)").bitcast(I32))
            return words

        def load_rows(src, a, c0):
            raw = ring.tile([P, PACK, KP], F32, name="raw", tag="raw", bufs=3)
            nc.sync.dma_start(raw[:], src[KP * a : KP * (a + 1), c0 : c0 + KP].rearrange("(p j) c -> p j c", j=PACK))
            return raw

        nc.sync.dma_start(idx[:], offs)
        nc.sync.dma_start(tab_s[:32, :].bitcast(I32), tab_scales.rearrange("a q t -> q a t").bitcast(I32))
        tab_w = [load_table_words(a) for a in range(PASSES)]
        w1_raw = {}
        for a in range(PASSES):
            w1_raw[a, 0] = load_rows(w1, a, 0)
        effort_t = keep.tile([P, PASSES, PACK], F32, name="effort_t")
        nc.sync.dma_start(effort_t[:], effort.rearrange("(b p i) -> p b i", b=PASSES, i=PACK))
        nc.sync.dma_start(idx2[:], offs2)
        wgs_t = keep.tile([P, S], F32, name="wgs_t")
        nc.sync.dma_start(wgs_t[:], wgs)
        nc.sync.dma_start(idx3[:], offs3)
        wgt_t = keep.tile([P, M], F32, name="wgt_t")
        nc.sync.dma_start(wgt_t[:], wgt)
        relief_t = keep.tile([P, PASSES, PACK], F32, name="relief_t")
        nc.sync.dma_start(relief_t[:], relief.rearrange("(b p i) -> p b i", b=PASSES, i=PACK))

        v_w = [keep.tile([P, S], U32, name=f"v_w{a}", align_bytes=64) for a in range(PASSES)]
        picked_s = keep.tile([P, S], U8, name="picked_s", align_bytes=64)
        nc.vector.tensor_copy(picked_s[:], tab_s[:].indirect(idx[:]))
        for q in range(4):
            nc.scalar.dma_start(
                v_s[32 * q : 32 * q + 4, :, :].bitcast(I32), picked_s[8 * q : 8 * q + 8, :].bitcast(I32)
            )
        for a in range(PASSES):
            nc.vector.tensor_copy(v_w[a][:], tab_w[a][:].indirect(idx[:]))

        def quantize(grouped, width, name):
            codes = keep.tile([P, width], U32, name=name + "_w", align_bytes=64)
            scales = keep.tile([P, width], U8, name=name + "_s", align_bytes=64)
            nc.vector.quantize_mx(out=codes[:].bitcast(FP8X4), scales=scales[:], in_=grouped)
            return codes, scales

        w1_q = {}

        def prepare_w1(b, u):
            head = (b, u) == (0, 0)
            grouped = ring.tile([P, PASSES, 2 * KP], BF16, name="grouped", tag="grouped", align_bytes=64)
            codes = keep.tile([P, PASSES, 2 * P], U32, name=f"w1q{b}{u}_w", align_bytes=64)
            scales = keep.tile([P, PASSES, 2 * P], U8, name=f"w1q{b}{u}_s", align_bytes=64)
            for a in range(PASSES):
                dst = grouped[:, a, :].rearrange("p (e m j) -> p m j e", e=2, j=PACK)
                src = w1_raw[a, b][:].rearrange("p j (m i) -> p m j i", i=PACK)[:, :, :, 2 * u : 2 * u + 2]
                if head:
                    nc.vector.tensor_copy(dst, src)
                    nc.vector.quantize_mx(out=codes[:, a, :].bitcast(FP8X4), scales=scales[:, a, :], in_=grouped[:, a, :])
                else:
                    nc.scalar.copy(dst, src)
            if not head:
                nc.vector.quantize_mx(
                    out=codes[:].rearrange("p a c -> p (a c)").bitcast(FP8X4),
                    scales=scales[:].rearrange("p a c -> p (a c)"),
                    in_=grouped[:].rearrange("p a c -> p (a c)"),
                )
            w1_q[b, u] = codes, scales

        def features(s):
            b, i = divmod(s, PACK)
            h = ring.tile([P, S], F32, name="h", tag="h")
            for c0 in range(0, S, BANK):
                cols = slice(c0, c0 + BANK)
                acc = psum.tile([P, BANK], F32, name="acc", tag="bank")
                for a in range(PASSES):
                    codes, scales = w1_q[b, i // 2]
                    rows = slice(P * (i % 2), P * (i % 2 + 1))
                    nc.tensor.matmul_mx(
                        out=acc[:],
                        lhsT=codes[:, a, rows].bitcast(FP8X4),
                        lhsT_scale=scales[:, a, rows],
                        rhs=v_w[a][:, cols].bitcast(FP8X4),
                        rhs_scale=v_s[:, a, cols],
                        start=(a == 0),
                        stop=(a == PASSES - 1),
                    )
                nc.scalar.activation(h[:, cols], acc[:], ACT.Copy, scale=effort_t[:, b, i : i + 1])
            return h

        def put(s, h):
            width = BANK if s == 0 else S
            for c0 in range(0, S, width):
                cols = slice(c0, c0 + width)
                window = pages[s % PAGES][:].indirect(idx2[:, c0 // 16 : (c0 + width) // 16])
                nc.vector.tensor_tensor(window, h[:, cols], wgs_t[:, cols], ALU.mult)

        act = [keep.tile([P, PACK, YW], F32, name=f"act{c0}") for c0 in range(0, M, YW)]
        act0 = keep.tile([P, PACK, M], F32, name="act_first", tag="act_first")
        ident = keep.tile([P, P], F32, name="ident")
        make_identity(nc, ident[:])
        turned = [keep.tile([P, M], F32, name=f"turned{u}", tag=f"turned{u}", align_bytes=64) for u in range(2)]
        x_last = []
        pain_t = []
        z_q = {}

        def read(s, c0, width):
            b, i = divmod(s, PACK)
            if s == SLICES - 1:
                x = sil = x_last[0][:, c0 : c0 + width]
            else:
                x = keep.tile([P, M], F32, name=f"x{s}", tag="x_spare" if s == SLICES - 2 else "x")
                if s > PACK:
                    sil = keep.tile([P, M], F32, name=f"sil{s}", tag=f"turned{SLICES - 2 - s}", align_bytes=64)
                else:
                    sil = ring.tile([P, M], F32, name="sil", tag="sil")
            window = pages[s % PAGES][:].indirect(idx3[:, c0 // 16 : (c0 + width) // 16])
            nc.vector.tensor_tensor(x[:], window, wgt_t[:, c0 : c0 + width], ALU.mult)
            nc.scalar.activation(sil[:], x[:], ACT.Silu)
            gain = relief_t[:, b, i : i + 1]
            if b == 0:
                nc.scalar.activation(act0[:, i, :], sil[:], ACT.Copy, scale=gain)
            else:
                for d0 in range(0, width, YW):
                    nc.scalar.activation(act[(c0 + d0) // YW][:, i, :], sil[:, d0 : d0 + YW], ACT.Copy, scale=gain)

        def turn_pair(u):
            for t0 in range(0, M, 2 * P):
                sums = psum.tile([P, 2, 2, P], F32, name="sums", tag="bank")
                for t in range(2):
                    cols = slice(t0 + P * t, t0 + P * (t + 1))
                    for e in range(2):
                        for first, src in ((True, pain_t[0]), (False, act0)):
                            nc.tensor.matmul(
                                sums[:, t, e, :], src[:, 2 * u + e, cols], ident[:], start=first, stop=not first, is_transpose=True
                            )
                nc.scalar.copy(
                    turned[u][:, t0 : t0 + 2 * P].bitcast(BF16).rearrange("m (t p e) -> m t p e", t=2, e=2),
                    sums[:].rearrange("m t e p -> m t p e"),
                )

        def weave_z0():
            zb = ring.tile([P, M * PACK], BF16, name="zb0", tag="grouped", align_bytes=64)
            for t0 in range(0, M, 2 * P):
                back = psum.tile([P, 2, 2, P], F32, name="back", tag="bank")
                for t in range(2):
                    for u in range(2):
                        nc.tensor.transpose(back[:, t, u, :], turned[u][:, t0 + P * t : t0 + P * (t + 1)], ident[:])
                nc.scalar.copy(
                    zb[:, PACK * t0 : PACK * (t0 + 2 * P)].bitcast(F32).rearrange("p (t m u) -> p t m u", t=2, u=2),
                    back[:].rearrange("p t u m -> p t m u"),
                )
            return zb

        def make_z(b, c):
            zb = keep.tile([P, YW * PACK], BF16, name=f"zb{b}_{c}", align_bytes=64)
            nc.vector.tensor_tensor(
                zb[:].rearrange("p (m e i) -> p m i e", e=2, i=PACK),
                act[c][:].rearrange("p i (m e) -> p m i e", e=2),
                pain_t[b][:, :, c * YW : (c + 1) * YW].rearrange("p i (m e) -> p m i e", e=2),
                ALU.add,
            )
            return zb

        def quantize_z(b, c, zb):
            z_q[b, c] = quantize(zb[:], CHUNK[b], f"zq{b}_{c}")

        prepare_w1(0, 0)
        h = {0: features(0)}
        h[1] = features(1)
        prepare_w1(0, 1)

        for a in range(PASSES):
            w1_raw[a, 1] = load_rows(w1, a, KP)
        wb_raw = []
        for b in range(PASSES):
            rows = ring.tile([P, PACK, M], F32, name=f"pain{b}", tag="big")
            nc.sync.dma_start(rows[:], pain[KP * b : KP * (b + 1), :].rearrange("(p i) m -> p i m", i=PACK))
            pain_t.append(rows)
            if b == 0:
                wb_raw.extend(load_rows(wb, a, 0) for a in range(PASSES))
        wa_w = keep.tile([P, PASSES, 2 * N], U8, name="wa_w", align_bytes=64)
        nc.sync.dma_start(wa_w[:].bitcast(I32), wa_words.rearrange("a p c -> p a c").bitcast(I32))
        for q in range(4):
            nc.sync.dma_start(
                wa_s[32 * q : 32 * q + 4, :, :].bitcast(I32),
                wa_scales[:, 4 * q : 4 * q + 4, :].rearrange("a r c -> r a c").bitcast(I32),
            )
        ba_t = keep.tile([P, N // P], F32, name="ba_t")
        with nc.allow_non_contiguous_dma(reason="one bias value a partition"):
            nc.sync.dma_start(ba_t[:], ba.rearrange("(t p) -> p t", p=P))

        def prepare_wb():
            grouped = ring.tile([P, PASSES, PACK * N], BF16, name="wb_grouped", tag="grouped", align_bytes=64)
            for b in range(PASSES):
                nc.scalar.copy(
                    grouped[:, b, :].rearrange("p (n e j) -> p n j e", e=2, j=PACK),
                    wb_raw[b][:].rearrange("p j (n e) -> p n j e", e=2),
                )
            return quantize(grouped[:].rearrange("p b c -> p (b c)"), PASSES * N, "wbq")

        put(0, h[0])
        for s in range(1, SLICES):
            if s + 1 < SLICES:
                h[s + 1] = features(s + 1)
            if s == SLICES - 2:
                turn_pair(1)
                zb0 = weave_z0()
            put(s, h[s])
            read(s - 1, 0, M)
            if s == 1:
                prepare_w1(1, 0)
                prepare_w1(1, 1)
            if s == 2:
                wb_w, wb_s = prepare_wb()
            if s == 3:
                turn_pair(0)
        quantize_z(0, 0, zb0)
        x_last.append(keep.tile([P, M], F32, name="x_last", tag="turned1", align_bytes=64))

        chunks = M // YW
        banks = {}
        scores = keep.tile([P, 2 * chunks, 2 * YW], F32, name="scores", tag="act_first")

        def z_operand(b, c, lo, width):
            per = CHUNK[b] // YW
            codes, scales = z_q[b, c // per]
            cols = slice((c % per) * YW + lo, (c % per) * YW + lo + width)
            return codes[:, cols].bitcast(FP8X4), scales[:, cols]

        def products(b, c):
            for pair in range(2):
                if b == 0:
                    banks[c, pair] = [psum.tile([P, 2, YW], F32, name=name, tag="bank") for name in ("ya", "yb")]
                ya, yb = banks[c, pair]
                for j in range(2):
                    n0 = P * (2 * pair + j)
                    for lo in range(0, YW, P):
                        rhs, rhs_scale = z_operand(b, c, lo, P)
                        nc.tensor.matmul_mx(
                            out=ya[:, j, lo : lo + P],
                            lhsT=wa_w[:, b, 2 * n0 : 2 * (n0 + P)].bitcast(FP4X4),
                            lhsT_scale=wa_s[:, b, n0 : n0 + P],
                            rhs=rhs,
                            rhs_scale=rhs_scale,
                            start=(b == 0 and j == 0 and lo == 0),
                            stop=(b == PASSES - 1 and j == 1 and lo == YW - P),
                        )
                for j in range(2):
                    n0 = P * (2 * pair + j)
                    rhs, rhs_scale = z_operand(b, c, 0, YW)
                    nc.tensor.matmul_mx(
                        out=yb[:, j, :],
                        lhsT=wb_w[:, N * b + n0 : N * b + n0 + P].bitcast(FP8X4),
                        lhsT_scale=wb_s[:, N * b + n0 : N * b + n0 + P],
                        rhs=rhs,
                        rhs_scale=rhs_scale,
                        start=(b == 0 and j == 0),
                        stop=(b == PASSES - 1 and j == 1),
                    )

        def finish(c):
            for pair in range(2):
                ya, yb = banks[c, pair]
                biased = scores[:, 2 * c + pair, :].rearrange("p (j m) -> p j m", j=2)
                for j in range(2):
                    t = 2 * pair + j
                    nc.scalar.activation(biased[:, j, :], ya[:, j, :], ACT.Identity, bias=ba_t[:, t : t + 1])
                nc.vector.tensor_tensor(biased, yb[:], biased, ALU.min)
                nc.sync.dma_start(
                    out[2 * P * pair : 2 * P * (pair + 1), c * YW : (c + 1) * YW].rearrange("(j p) m -> p j m", p=P), biased
                )

        products(0, 0)
        products(0, 1)
        last = SLICES - 1
        zb = {}

        def close(c):
            quantize_z(1, c, zb[c])
            if c >= 2:
                products(0, c)
            products(1, c)

        for c in range(3):
            read(last, c * YW, YW)
        zb[0] = make_z(1, 0)
        read(last, 3 * YW, YW)
        close(0)
        zb[1] = make_z(1, 1)
        close(1)
        zb[2] = make_z(1, 2)
        finish(0)
        close(2)
        finish(1)
        zb[3] = make_z(1, 3)
        close(3)
        finish(2)
        finish(3)
